import numpy as np
import ml_dtypes


def mxq(x, axis, fmt="e4m3"):
    dtype, down = {"e4m3": (ml_dtypes.float8_e4m3fn, 7), "e5m2": (ml_dtypes.float8_e5m2, 14)}[fmt]
    v = np.moveaxis(np.asarray(x, np.float32).astype(ml_dtypes.bfloat16).astype(np.float64), axis, -1)
    blocks = v.reshape(v.shape[:-1] + (-1, 32))
    amax = np.abs(blocks).max(-1, keepdims=True)
    byte = np.maximum(np.where(amax > 0, np.frexp(amax)[1] - 1 + 127, 0) - down, 1)
    scale = np.exp2(byte - 127.0)
    codes = (blocks / scale).astype(np.float32).astype(dtype).astype(np.float64)
    return np.moveaxis((codes * scale).reshape(v.shape), -1, axis)


WIDE = False


def mx_kscale(k):
    if not WIDE:
        return np.ones(k)
    levels = np.array([10, -10, 5, -5, 0])
    if k % 512:
        return np.exp2(np.random.permutation(np.resize(levels, k // 32))).repeat(32)
    a = np.empty((k // 512, 16))
    for p in range(k // 512):
        a[p, :8] = np.random.permutation(np.resize(levels, 8))
        for g in range(8):
            far = levels[np.abs(levels - a[p, g]) >= 10]
            a[p, g + 8] = far[np.random.randint(len(far))]
    return np.exp2(a.ravel()).repeat(32)


def f64(x):
    return np.asarray(x).astype(np.float64)


def striped(idx):
    return np.tile(idx.reshape(-1, 16).T, (8, 1)).astype(np.uint16)


def unstriped(offs):
    return offs[:16].T.reshape(-1).astype(np.int64)


def striped8(idx):
    return np.concatenate([x.reshape(-1, 16).T for x in idx]).astype(np.uint16)


def runs(offs, k):
    lists = np.stack([offs[16 * r : 16 * r + 16].T.reshape(-1) for r in range(8)]).astype(np.int64)
    return lists[np.arange(k) % 512 // 64]


def pack_weight(w):
    k, n = w.shape
    w = f64(np.asarray(w, np.float32).astype(ml_dtypes.bfloat16)).reshape(k // 32, 32, n)
    amax = np.abs(w).max(1)
    byte = np.clip(np.where(amax > 0, np.frexp(amax)[1] - 1 + 127 - 7, 1), 1, 254)
    scaled = (w * np.exp2(127.0 - byte)[:, None, :]).reshape(k, n).astype(np.float32)
    words = np.ascontiguousarray(scaled.reshape(k // 512, 128, 4, n).transpose(0, 1, 3, 2)).astype(ml_dtypes.float8_e4m3fn).view(np.uint8)
    return words, np.ascontiguousarray(byte.astype(np.uint8).reshape(k // 512, 16, n))


def unpack_weight(words, scales):
    g, p, n, _ = words.shape
    vals = np.ascontiguousarray(words).view(ml_dtypes.float8_e4m3fn).astype(np.float64) * np.repeat(np.exp2(scales.astype(np.float64) - 127.0), 8, axis=1)[..., None]
    return vals.transpose(0, 1, 3, 2).reshape(g * 512, n)


E2M1 = np.array([0.0, 0.5, 1.0, 1.5, 2.0, 3.0, 4.0, 6.0, -0.0, -0.5, -1.0, -1.5, -2.0, -3.0, -4.0, -6.0])


def pack_fp4(w):
    k, n = w.shape
    w = f64(np.asarray(w, np.float32).astype(ml_dtypes.bfloat16)).reshape(k // 32, 32, n)
    amax = np.abs(w).max(1)
    mant, ex = np.frexp(amax / 6.0)
    byte = np.clip(np.where(amax > 0, np.where(mant > 0.5, ex, ex - 1) + 127, 1), 1, 254)
    scaled = (w * np.exp2(127.0 - byte)[:, None, :]).reshape(k, n).astype(np.float32)
    c = np.ascontiguousarray(scaled.reshape(k // 512, 128, 4, n).transpose(0, 1, 3, 2)).astype(ml_dtypes.float4_e2m1fn).view(np.uint8) & 0xF
    words = (c[..., 0::2] | (c[..., 1::2] << 4)).reshape(k // 512, 128, 2 * n)
    return np.ascontiguousarray(words), np.ascontiguousarray(byte.astype(np.uint8).reshape(k // 512, 16, n))


def unpack_fp4(words, scales):
    g, _, n = scales.shape
    words = np.ascontiguousarray(words).reshape(g, 128, n, 2)
    nib = np.empty((g, 128, n, 4), np.uint8)
    nib[..., 0::2] = words & 0xF
    nib[..., 1::2] = words >> 4
    vals = E2M1[nib] * np.repeat(np.exp2(scales.astype(np.float64) - 127.0), 8, axis=1)[..., None]
    return vals.transpose(0, 1, 3, 2).reshape(g * 512, n)


def planes(y):
    n, m = y.shape
    v = y.astype(np.float32).astype(ml_dtypes.bfloat16).astype(np.float64).reshape(n // 32, 32, m)
    top = np.abs(v).max(1)
    byte = np.clip(np.where(top > 0, np.frexp(top)[1] - 1 + 127 - 7, 1), 1, 254)
    codes = (v * np.exp2(127.0 - byte)[:, None, :]).reshape(n, m).astype(np.float32).astype(ml_dtypes.float8_e4m3fn).view(np.uint8)
    words = codes.reshape(n // 512, 128, 4, m).transpose(0, 1, 3, 2)
    return np.ascontiguousarray(words), np.ascontiguousarray(byte.astype(np.uint8).reshape(n // 512, 16, m))


K, T, S, N, H = 512, 2048, 512, 512, 512


def setup_inputs():
    n = np.random.standard_normal
    s = mx_kscale(K)[:, None]
    u = mx_kscale(S)
    packed_xT = pack_weight(n((K, T)) * s)
    packed_w1 = pack_fp4(n((S, N)) / np.sqrt(S) / u[:, None])
    return {
        "x_words": packed_xT[0],
        "x_scales": packed_xT[1],
        "wa": (n((K, H)) / np.sqrt(K) / s).astype(np.float32),
        "gt": (np.random.uniform(0.5, 1.5, (S, 1)) * u[:, None]).astype(np.float32),
        "w1_words": packed_w1[0],
        "w1_scales": packed_w1[1],
        "offs": striped(np.random.permutation(T)[:S]),
        "fa": striped8(np.stack([np.random.permutation(H) for _ in range(8)])),
        "fb": striped8(np.stack([np.random.permutation(H) for _ in range(8)])),
    }


def reference(x_words, x_scales, wa, gt, w1_words, w1_scales, offs, fa, fb):
    xq = unpack_weight(x_words, x_scales)[:, unstriped(offs)]
    y = xq.T @ mxq(f64(wa), 0, "e4m3")
    a = y[np.arange(S)[:, None], runs(fa, S)]
    b = y[np.arange(S)[:, None], runs(fb, S)]
    z = f64(gt) * (np.maximum(np.minimum(y, a), np.minimum(np.maximum(y, a), b)))
    out_0 = unpack_fp4(w1_words, w1_scales).T @ mxq(z, 0, "e4m3")
    return (out_0,) + planes(out_0)

@@ -1,0 +1,221 @@
+from contextlib import ExitStack
+
+import concourse.mybir as mybir
+
+F32 = mybir.dt.float32
+BF16 = mybir.dt.bfloat16
+I32 = mybir.dt.int32
+U32 = mybir.dt.uint32
+U16 = mybir.dt.uint16
+U8 = mybir.dt.uint8
+FP8X4 = mybir.dt.float8_e4m3fn_x4
+FP4X4 = mybir.dt.float4_e2m1fn_x4
+MIN = mybir.AluOpType.min
+MAX = mybir.AluOpType.max
+COPY = mybir.ActivationFunctionType.Copy
+
+P = 128
+PACK = 4
+K, T, S, H, N = 512, 2048, 512, 512, 512
+LANES = 16
+HALF = H // 2
+QUARTER = H // 4
+FLOPS = 2 * K * S * H + 2 * S * N * H
+
+
+def weave(copy, dst, src):
+    copy(
+        dst.rearrange("p (c i t) -> p c t i", i=4, t=PACK),
+        src.rearrange("p t (c i) -> p c t i", i=4),
+    )
+
+
+def tile_picked_featmed_none_po_kernel(
+    tc, x_words, x_scales, wa, gt, w1_words, w1_scales, offs, fa, fb, out_0, out_1, out_2
+):
+    nc = tc.nc
+    with ExitStack() as ctx:
+        lists = ctx.enter_context(tc.tile_pool(name="lists", bufs=1))
+        keep = ctx.enter_context(tc.tile_pool(name="keep", bufs=1))
+        psum = ctx.enter_context(tc.psum_pool(name="psum", bufs=8))
+        sc, vc = nc.scalar.copy, nc.vector.tensor_copy
+
+        def sb(name, shape, dtype, tag=""):
+            return keep.tile(shape, dtype, name=name, tag=tag or name, align_bytes=64)
+
+        def bank(name):
+            return psum.tile([P, 512], F32, name=name, tag="bank")
+
+        offs_sb = lists.tile([P, S // LANES], U16, name="offs_sb")
+        fa_sb = lists.tile([P, H // LANES], U16, name="fa_sb")
+        fb_sb = lists.tile([P, H // LANES], U16, name="fb_sb")
+
+        xs_raw = sb("xs_raw", [P, T], U8)
+        w1s_raw = sb("w1s_raw", [P, N], U8)
+        nc.gpsimd.memset(xs_raw[:].bitcast(I32), 0)
+        nc.gpsimd.memset(w1s_raw[:].bitcast(I32), 0)
+        wa_rows = wa.rearrange("(p j) h -> p j h", j=PACK)
+        wa_raw = [sb("wa_raw%d" % n, [P, PACK, HALF], F32) for n in range(2)]
+        xw_raw = sb("xw_raw", [P, T], U32)
+        gt_sb = sb("gt_sb", [P, PACK], F32)
+        w1w_raw = sb("w1w_raw", [P, 2 * N], U8)
+
+        nc.sync.dma_start(wa_raw[0][:], wa_rows[:, :, 0:HALF])
+        for q in range(4):
+            nc.sync.dma_start(xs_raw[32 * q : 32 * q + 4, :].bitcast(I32), x_scales[0, 4 * q : 4 * q + 4, :].bitcast(I32))
+        nc.sync.dma_start(offs_sb[:], offs)
+        nc.sync.dma_start(wa_raw[1][:], wa_rows[:, :, HALF:H])
+        nc.sync.dma_start(xw_raw[:].bitcast(I32), x_words[0].rearrange("p n t -> p (n t)").bitcast(I32))
+        nc.sync.dma_start(gt_sb[:], gt.rearrange("(p t) o -> p (t o)", t=PACK))
+        nc.sync.dma_start(fa_sb[:], fa)
+        nc.sync.dma_start(fb_sb[:], fb)
+        nc.sync.dma_start(w1w_raw[:].bitcast(I32), w1_words[0].bitcast(I32))
+        for q in range(4):
+            nc.sync.dma_start(w1s_raw[32 * q : 32 * q + 4, :].bitcast(I32), w1_scales[0, 4 * q : 4 * q + 4, :].bitcast(I32))
+
+        xs_picked = sb("xs_picked", [P, S], U8)
+        xs = sb("xs", [P, S], U8)
+        xw = sb("xw", [P, S], U32)
+        w1w = sb("w1w", [P, 2 * N], U8)
+        w1s = sb("w1s", [P, N], U8)
+        wa16 = [sb("wa16_%d" % n, [P, PACK * HALF], BF16) for n in range(2)]
+        wa_codes = [sb("wa_codes%d" % n, [P, HALF], U32) for n in range(2)]
+        wa_scales = [sb("wa_scales%d" % n, [P, HALF], U8) for n in range(2)]
+        y32 = [sb("y32_%d" % t, [P, H], F32) for t in range(PACK)]
+        y16 = sb("y16", [P, PACK, H], BF16)
+
+        def quant_wa(n):
+            nc.vector.quantize_mx(out=wa_codes[n][:].bitcast(FP8X4), scales=wa_scales[n][:], in_=wa16[n][:])
+
+        def first(acc, t, n):
+            rows = slice(P * t, P * (t + 1))
+            nc.tensor.matmul_mx(
+                out=acc, lhsT=xw[:, rows].bitcast(FP8X4), lhsT_scale=xs[:, rows],
+                rhs=wa_codes[n][:].bitcast(FP8X4), rhs_scale=wa_scales[n][:], start=True, stop=True,
+            )
+
+        weave(sc, wa16[0][:], wa_raw[0][:])
+        weave(sc, wa16[1][:], wa_raw[1][:])
+        vc(xs_picked[:], xs_raw[:].indirect(offs_sb[:]))
+        quant_wa(0)
+        vc(xs[:].rearrange("p (t m) -> p t m", t=PACK), xs_picked[:].rearrange("p (m t) -> p t m", t=PACK))
+        quant_wa(1)
+        vc(xw[:].rearrange("p (t m) -> p m t", t=PACK), xw_raw[:].indirect(offs_sb[:]))
+        vc(
+            w1w[:].rearrange("p (t m b) -> p t m b", t=PACK, b=2),
+            w1w_raw[:].rearrange("p (m t b) -> p t m b", t=PACK, b=2),
+        )
+        vc(w1s[:].rearrange("p (t m) -> p t m", t=PACK), w1s_raw[:].rearrange("p (m t) -> p t m", t=PACK))
+        for t in range(PACK):
+            acc = bank("y_acc%d" % t)
+            for n in range(2):
+                first(acc[:, HALF * n : HALF * (n + 1)], t, n)
+            nc.scalar.activation(y32[t][:], acc[:], COPY, scale=gt_sb[:, t : t + 1])
+        for t in range(PACK):
+            sc(y16[:, t, :], y32[t][:])
+
+        out_rows = out_0.rearrange("(p t) h -> p t h", t=PACK)
+        out_words = out_1[0].rearrange("p n t -> p (n t)").bitcast(I32)
+        o_scales = sb("o_scales", [P, H], U8)
+
+        def gather(dst, lst, t, c0, c1):
+            nc.vector.tensor_copy(dst, y32[t][:].indirect(lst[:, c0 // LANES : c1 // LANES]))
+
+        def pick(dst, u, v, op):
+            nc.vector.tensor_tensor(dst, u, v, op)
+
+        def quant_z(name, zw, w):
+            zc = sb(name + "_codes", [P, w], U32)
+            zs = sb(name + "_scales", [P, w], U8)
+            nc.vector.quantize_mx(out=zc[:].bitcast(FP8X4), scales=zs[:], in_=zw[:])
+            return zc, zs
+
+        def second(name, zq, c0, c1, copies):
+            w = c1 - c0
+            o32 = sb(name, [P, PACK, w], F32)
+            for half in range(2):
+                acc = bank("%s_acc%d" % (name, half))
+                for u in range(2):
+                    t = 2 * half + u
+                    nc.tensor.matmul_mx(
+                        out=acc[:, u * w : (u + 1) * w],
+                        lhsT=w1w[:, 2 * P * t : 2 * P * (t + 1)].bitcast(FP4X4),
+                        lhsT_scale=w1s[:, P * t : P * (t + 1)],
+                        rhs=zq[0][:].bitcast(FP8X4), rhs_scale=zq[1][:], start=True, stop=True,
+                    )
+                copies[half](o32[:, 2 * half : 2 * half + 2, :].rearrange("p t w -> p (t w)"), acc[:, 0 : 2 * w])
+            nc.sync.dma_start(out_rows[:, :, c0:c1], o32[:])
+            return o32
+
+        def round_out(name, copy, o32, w):
+            o16 = sb(name, [P, PACK * w], BF16)
+            weave(copy, o16[:], o32[:])
+            return o16
+
+        def quant_out(name, o16, c0, c1):
+            oc = sb(name, [P, c1 - c0], U32)
+            nc.vector.quantize_mx(out=oc[:].bitcast(FP8X4), scales=o_scales[:, c0:c1], in_=o16[:])
+            nc.sync.dma_start(out_words[:, c0:c1], oc[:].bitcast(I32))
+
+        q3 = HALF + QUARTER
+        pairs = (slice(0, 2), slice(2, 4))
+        a0 = sb("a0", [P, PACK, HALF], BF16)
+        b0 = sb("b0", [P, PACK, HALF], BF16, "picked")
+        hi0 = sb("hi0", [P, PACK, HALF], BF16)
+        lo0 = sb("lo0", [P, PACK, HALF], BF16)
+        z0 = sb("z0", [P, PACK, HALF], BF16, "z0")
+        for t in range(PACK):
+            gather(a0[:, t, :], fa_sb, t, 0, HALF)
+            gather(b0[:, t, :], fb_sb, t, 0, HALF)
+        pick(hi0[:], y16[:, :, 0:HALF], a0[:], MAX)
+        pick(lo0[:], y16[:, :, 0:HALF], a0[:], MIN)
+        for ts in pairs:
+            pick(hi0[:, ts, :], hi0[:, ts, :], b0[:, ts, :], MIN)
+        for ts in pairs:
+            pick(z0[:, ts, :], hi0[:, ts, :], lo0[:, ts, :], MAX)
+        zw0 = sb("zw0", [P, PACK * HALF], BF16)
+        weave(sc, zw0[:], z0[:])
+        a1 = sb("a1", [P, PACK, HALF], BF16, "picked")
+        for t in range(PACK):
+            gather(a1[:, t, :], fa_sb, t, HALF, H)
+        zq0 = quant_z("zq0", zw0, HALF)
+        o0 = second("o0", zq0, 0, HALF, (sc, sc))
+        o16_0 = round_out("o16_0", sc, o0, HALF)
+
+        work = sb("work", [P, 3, PACK, HALF], BF16, "z0")
+        hi1, lo1 = work[:, 0], work[:, 1]
+        b1 = work[:, 2].rearrange("p t w -> p (t w)")[:, 0 : PACK * QUARTER].rearrange("p (t w) -> p t w", t=PACK)
+        pick(hi1, y16[:, :, HALF:H], a1[:], MAX)
+        pick(lo1, y16[:, :, HALF:H], a1[:], MIN)
+        for t in range(PACK):
+            gather(b1[:, t, :], fb_sb, t, HALF, q3)
+        b2a = sb("b2a", [P, 3, QUARTER], BF16, "picked")
+        gather(b2a[:, 0, :], fb_sb, 0, q3, H)
+        pick(hi1[:, :, 0:QUARTER], hi1[:, :, 0:QUARTER], b1, MIN)
+        gather(b2a[:, 1, :], fb_sb, 1, q3, H)
+        z1 = sb("z1", [P, PACK, QUARTER], BF16, "z1")
+        pick(z1[:], hi1[:, :, 0:QUARTER], lo1[:, :, 0:QUARTER], MAX)
+        zw1 = sb("zw1", [P, PACK * QUARTER], BF16)
+        weave(sc, zw1[:], z1[:])
+        gather(b2a[:, 2, :], fb_sb, 2, q3, H)
+        quant_out("oc0", o16_0, 0, HALF)
+        pick(hi1[:, 0:3, QUARTER:], hi1[:, 0:3, QUARTER:], b2a[:], MIN)
+        zq1 = quant_z("zq1", zw1, QUARTER)
+        o1 = second("o1", zq1, HALF, q3, (sc, sc))
+        o16_1 = round_out("o16_1", sc, o1, QUARTER)
+        last = sb("last", [P, PACK + 1, QUARTER], BF16, "z1")
+        z2, b2b = last[:, 0:PACK, :], last[:, PACK, :]
+        gather(b2b, fb_sb, 3, q3, H)
+        pick(z2[:, 0:3, :], hi1[:, 0:3, QUARTER:], lo1[:, 0:3, QUARTER:], MAX)
+        pick(hi1[:, 3, QUARTER:], hi1[:, 3, QUARTER:], b2b, MIN)
+        pick(z2[:, 3, :], hi1[:, 3, QUARTER:], lo1[:, 3, QUARTER:], MAX)
+        zw2 = sb("zw2", [P, PACK * QUARTER], BF16)
+        weave(vc, zw2[:], z2)
+        zq2 = quant_z("zq2", zw2, QUARTER)
+        quant_out("oc1", o16_1, HALF, q3)
+        o2 = second("o2", zq2, q3, H, (sc, vc))
+        o16_2 = round_out("o16_2", vc, o2, QUARTER)
+        quant_out("oc2", o16_2, q3, H)
+        for q in range(4):
+            eng = nc.scalar if q % 2 else nc.sync
+            eng.dma_start(out_2[0, 4 * q : 4 * q + 4, :].bitcast(I32), o_scales[32 * q : 32 * q + 4, :].bitcast(I32))

@@ -51,25 +51,25 @@ def tile_picked_featmed_none_po_kernel(
         fb_sb = lists.tile([P, H // LANES], U16, name="fb_sb")
 
         xs_raw = sb("xs_raw", [P, T], U8)
+        gt_sb = sb("gt_sb", [P, PACK], F32)
         w1s_raw = sb("w1s_raw", [P, N], U8)
-        nc.gpsimd.memset(xs_raw[:].bitcast(I32), 0)
+        nc.vector.memset(xs_raw[:].bitcast(I32), 0)
+        nc.gpsimd.dma_start(gt_sb[:], gt.rearrange("(p t) o -> p (t o)", t=PACK))
         nc.gpsimd.memset(w1s_raw[:].bitcast(I32), 0)
         wa_rows = wa.rearrange("(p j) h -> p j h", j=PACK)
         wa_raw = [sb("wa_raw%d" % n, [P, PACK, HALF], F32) for n in range(2)]
         xw_raw = sb("xw_raw", [P, T], U32)
-        gt_sb = sb("gt_sb", [P, PACK], F32)
         w1w_raw = sb("w1w_raw", [P, 2 * N], U8)
 
-        nc.sync.dma_start(wa_raw[0][:], wa_rows[:, :, 0:HALF])
-        for q in range(4):
-            nc.sync.dma_start(xs_raw[32 * q : 32 * q + 4, :].bitcast(I32), x_scales[0, 4 * q : 4 * q + 4, :].bitcast(I32))
         nc.sync.dma_start(offs_sb[:], offs)
-        nc.sync.dma_start(wa_raw[1][:], wa_rows[:, :, HALF:H])
-        nc.sync.dma_start(xw_raw[:].bitcast(I32), x_words[0].rearrange("p n t -> p (n t)").bitcast(I32))
-        nc.sync.dma_start(gt_sb[:], gt.rearrange("(p t) o -> p (t o)", t=PACK))
         nc.sync.dma_start(fa_sb[:], fa)
-        nc.sync.dma_start(fb_sb[:], fb)
         nc.sync.dma_start(w1w_raw[:].bitcast(I32), w1_words[0].bitcast(I32))
+        nc.sync.dma_start(wa_raw[0][:], wa_rows[:, :, 0:HALF])
+        nc.sync.dma_start(fb_sb[:], fb)
+        nc.sync.dma_start(xw_raw[:].bitcast(I32), x_words[0].rearrange("p n t -> p (n t)").bitcast(I32))
+        nc.sync.dma_start(wa_raw[1][:], wa_rows[:, :, HALF:H])
+        for q in range(4):
+            nc.scalar.dma_start(xs_raw[32 * q : 32 * q + 4, :].bitcast(I32), x_scales[0, 4 * q : 4 * q + 4, :].bitcast(I32))
         for q in range(4):
             nc.sync.dma_start(w1s_raw[32 * q : 32 * q + 4, :].bitcast(I32), w1_scales[0, 4 * q : 4 * q + 4, :].bitcast(I32))
 
@@ -77,11 +77,9 @@ def tile_picked_featmed_none_po_kernel(
         xs = sb("xs", [P, S], U8)
         xw = sb("xw", [P, S], U32)
         w1w = sb("w1w", [P, 2 * N], U8)
-        w1s = sb("w1s", [P, N], U8)
         wa16 = [sb("wa16_%d" % n, [P, PACK * HALF], BF16) for n in range(2)]
         wa_codes = [sb("wa_codes%d" % n, [P, HALF], U32) for n in range(2)]
         wa_scales = [sb("wa_scales%d" % n, [P, HALF], U8) for n in range(2)]
-        y32 = [sb("y32_%d" % t, [P, H], F32) for t in range(PACK)]
         y16 = sb("y16", [P, PACK, H], BF16)
 
         def quant_wa(n):
@@ -94,19 +92,27 @@ def tile_picked_featmed_none_po_kernel(
                 rhs=wa_codes[n][:].bitcast(FP8X4), rhs_scale=wa_scales[n][:], start=True, stop=True,
             )
 
-        weave(sc, wa16[0][:], wa_raw[0][:])
-        weave(sc, wa16[1][:], wa_raw[1][:])
-        vc(xs_picked[:], xs_raw[:].indirect(offs_sb[:]))
-        quant_wa(0)
-        vc(xs[:].rearrange("p (t m) -> p t m", t=PACK), xs_picked[:].rearrange("p (m t) -> p t m", t=PACK))
-        quant_wa(1)
-        vc(xw[:].rearrange("p (t m) -> p m t", t=PACK), xw_raw[:].indirect(offs_sb[:]))
         vc(
             w1w[:].rearrange("p (t m b) -> p t m b", t=PACK, b=2),
             w1w_raw[:].rearrange("p (m t b) -> p t m b", t=PACK, b=2),
         )
+        weave(sc, wa16[0][:], wa_raw[0][:])
+        vc(xs_picked[:], xs_raw[:].indirect(offs_sb[:]))
+        quant_wa(0)
+        vc(xs[:].rearrange("p (t m) -> p t m", t=PACK), xs_picked[:].rearrange("p (m t) -> p t m", t=PACK))
+        vc(xw[:].rearrange("p (t m) -> p m t", t=PACK), xw_raw[:].indirect(offs_sb[:]))
+        split = 96
+        weave(sc, wa16[1][:, 0 : PACK * split], wa_raw[1][:, :, 0:split])
+        weave(vc, wa16[1][:, PACK * split :], wa_raw[1][:, :, split:])
+        quant_wa(1)
+        w1s = sb("w1s", [P, N], U8, "wa16_1")
         vc(w1s[:].rearrange("p (t m) -> p t m", t=PACK), w1s_raw[:].rearrange("p (m t) -> p t m", t=PACK))
-        for t in range(PACK):
+        y32 = [sb("y32_%d" % t, [P, H], F32, "wa_raw1" if t == 0 else "") for t in range(PACK)]
+        for n in range(2):
+            acc = bank("y_acc0_%d" % n)
+            first(acc[:, 0:HALF], 0, n)
+            nc.scalar.activation(y32[0][:, HALF * n : HALF * (n + 1)], acc[:, 0:HALF], COPY, scale=gt_sb[:, 0:1])
+        for t in range(1, PACK):
             acc = bank("y_acc%d" % t)
             for n in range(2):
                 first(acc[:, HALF * n : HALF * (n + 1)], t, n)
@@ -207,15 +213,31 @@ def tile_picked_featmed_none_po_kernel(
         z2, b2b = last[:, 0:PACK, :], last[:, PACK, :]
         gather(b2b, fb_sb, 3, q3, H)
         pick(z2[:, 0:3, :], hi1[:, 0:3, QUARTER:], lo1[:, 0:3, QUARTER:], MAX)
-        pick(hi1[:, 3, QUARTER:], hi1[:, 3, QUARTER:], b2b, MIN)
-        pick(z2[:, 3, :], hi1[:, 3, QUARTER:], lo1[:, 3, QUARTER:], MAX)
+        eighth = QUARTER // 2
+        parts = (slice(0, eighth), slice(eighth, QUARTER))
+        woven = [slice(PACK * c.start, PACK * c.stop) for c in parts]
+        hi2, lo2 = hi1[:, 3, QUARTER:], lo1[:, 3, QUARTER:]
+        for c in parts:
+            pick(hi2[:, c], hi2[:, c], b2b[:, c], MIN)
+        for c in parts:
+            pick(z2[:, 3, c], hi2[:, c], lo2[:, c], MAX)
         zw2 = sb("zw2", [P, PACK * QUARTER], BF16)
-        weave(vc, zw2[:], z2)
-        zq2 = quant_z("zq2", zw2, QUARTER)
+        for c, cw in zip(parts, woven):
+            weave(vc, zw2[:, cw], z2[:, :, c])
+        zq2 = (sb("zq2_codes", [P, QUARTER], U32), sb("zq2_scales", [P, QUARTER], U8))
+        for c, cw in zip(parts, woven):
+            nc.vector.quantize_mx(out=zq2[0][:, c].bitcast(FP8X4), scales=zq2[1][:, c], in_=zw2[:, cw])
         quant_out("oc1", o16_1, HALF, q3)
-        o2 = second("o2", zq2, q3, H, (sc, vc))
-        o16_2 = round_out("o16_2", vc, o2, QUARTER)
-        quant_out("oc2", o16_2, q3, H)
+        o2 = second("o2", zq2, q3, H, (vc, sc))
+        o16_2 = sb("o16_2", [P, PACK * QUARTER], BF16)
+        for c, cw in zip(parts, woven):
+            weave(vc, o16_2[:, cw], o2[:, :, c])
+        oc2 = sb("oc2", [P, QUARTER], U32)
+        for c, cw in zip(parts, woven):
+            nc.vector.quantize_mx(
+                out=oc2[:, c].bitcast(FP8X4), scales=o_scales[:, q3 + c.start : q3 + c.stop], in_=o16_2[:, cw]
+            )
+        nc.sync.dma_start(out_words[:, q3:H], oc2[:].bitcast(I32))
         for q in range(4):
             eng = nc.scalar if q % 2 else nc.sync
             eng.dma_start(out_2[0, 4 * q : 4 * q + 4, :].bitcast(I32), o_scales[32 * q : 32 * q + 4, :].bitcast(I32))

@@ -71,7 +71,8 @@ def tile_picked_featmed_none_po_kernel(
         for q in range(4):
             nc.scalar.dma_start(xs_raw[32 * q : 32 * q + 4, :].bitcast(I32), x_scales[0, 4 * q : 4 * q + 4, :].bitcast(I32))
         for q in range(4):
-            nc.sync.dma_start(w1s_raw[32 * q : 32 * q + 4, :].bitcast(I32), w1_scales[0, 4 * q : 4 * q + 4, :].bitcast(I32))
+            queue = nc.gpsimd if q == 3 else nc.sync
+            queue.dma_start(w1s_raw[32 * q : 32 * q + 4, :].bitcast(I32), w1_scales[0, 4 * q : 4 * q + 4, :].bitcast(I32))
 
         xs_picked = sb("xs_picked", [P, S], U8)
         xs = sb("xs", [P, S], U8)
@@ -100,10 +101,15 @@ def tile_picked_featmed_none_po_kernel(
         vc(xs_picked[:], xs_raw[:].indirect(offs_sb[:]))
         quant_wa(0)
         vc(xs[:].rearrange("p (t m) -> p t m", t=PACK), xs_picked[:].rearrange("p (m t) -> p t m", t=PACK))
-        vc(xw[:].rearrange("p (t m) -> p m t", t=PACK), xw_raw[:].indirect(offs_sb[:]))
-        split = 96
+        xw_picked = sb("xw_picked", [P, S], U32)
+        vc(xw_picked[:], xw_raw[:].indirect(offs_sb[:]))
+        split = 160
         weave(sc, wa16[1][:, 0 : PACK * split], wa_raw[1][:, :, 0:split])
         weave(vc, wa16[1][:, PACK * split :], wa_raw[1][:, :, split:])
+        vc(
+            xw[:].bitcast(I32).rearrange("p (t c i) -> p c t i", t=PACK, i=4),
+            xw_picked[:].bitcast(I32).rearrange("p (c i t) -> p c t i", t=PACK, i=4),
+        )
         quant_wa(1)
         w1s = sb("w1s", [P, N], U8, "wa16_1")
         vc(w1s[:].rearrange("p (t m) -> p t m", t=PACK), w1s_raw[:].rearrange("p (m t) -> p t m", t=PACK))

from contextlib import ExitStack

import concourse.mybir as mybir

F32 = mybir.dt.float32
BF16 = mybir.dt.bfloat16
I32 = mybir.dt.int32
U32 = mybir.dt.uint32
U16 = mybir.dt.uint16
U8 = mybir.dt.uint8
FP8X4 = mybir.dt.float8_e4m3fn_x4
FP4X4 = mybir.dt.float4_e2m1fn_x4
MIN = mybir.AluOpType.min
MAX = mybir.AluOpType.max
COPY = mybir.ActivationFunctionType.Copy

P = 128
PACK = 4
K, T, S, H, N = 512, 2048, 512, 512, 512
LANES = 16
HALF = H // 2
QUARTER = H // 4
FLOPS = 2 * K * S * H + 2 * S * N * H


def weave(copy, dst, src):
    copy(
        dst.rearrange("p (c i t) -> p c t i", i=4, t=PACK),
        src.rearrange("p t (c i) -> p c t i", i=4),
    )


def tile_picked_featmed_none_po_kernel(
    tc, x_words, x_scales, wa, gt, w1_words, w1_scales, offs, fa, fb, out_0, out_1, out_2
):
    nc = tc.nc
    with ExitStack() as ctx:
        lists = ctx.enter_context(tc.tile_pool(name="lists", bufs=1))
        keep = ctx.enter_context(tc.tile_pool(name="keep", bufs=1))
        psum = ctx.enter_context(tc.psum_pool(name="psum", bufs=8))
        sc, vc = nc.scalar.copy, nc.vector.tensor_copy

        def sb(name, shape, dtype, tag=""):
            return keep.tile(shape, dtype, name=name, tag=tag or name, align_bytes=64)

        def bank(name):
            return psum.tile([P, 512], F32, name=name, tag="bank")

        offs_sb = lists.tile([P, S // LANES], U16, name="offs_sb")
        fa_sb = lists.tile([P, H // LANES], U16, name="fa_sb")
        fb_sb = lists.tile([P, H // LANES], U16, name="fb_sb")

        xs_raw = sb("xs_raw", [P, T], U8)
        gt_sb = sb("gt_sb", [P, PACK], F32)
        w1s_raw = sb("w1s_raw", [P, N], U8)
        nc.vector.memset(xs_raw[:].bitcast(I32), 0)
        nc.gpsimd.dma_start(gt_sb[:], gt.rearrange("(p t) o -> p (t o)", t=PACK))
        nc.gpsimd.memset(w1s_raw[:].bitcast(I32), 0)
        wa_rows = wa.rearrange("(p j) h -> p j h", j=PACK)
        wa_raw = [sb("wa_raw%d" % n, [P, PACK, HALF], F32) for n in range(2)]
        xw_raw = sb("xw_raw", [P, T], U32)
        w1w_raw = sb("w1w_raw", [P, 2 * N], U8)

        nc.sync.dma_start(offs_sb[:], offs)
        nc.sync.dma_start(fa_sb[:], fa)
        nc.sync.dma_start(w1w_raw[:].bitcast(I32), w1_words[0].bitcast(I32))
        nc.sync.dma_start(wa_raw[0][:], wa_rows[:, :, 0:HALF])
        nc.sync.dma_start(fb_sb[:], fb)
        nc.sync.dma_start(xw_raw[:].bitcast(I32), x_words[0].rearrange("p n t -> p (n t)").bitcast(I32))
        nc.sync.dma_start(wa_raw[1][:], wa_rows[:, :, HALF:H])
        for q in range(4):
            nc.scalar.dma_start(xs_raw[32 * q : 32 * q + 4, :].bitcast(I32), x_scales[0, 4 * q : 4 * q + 4, :].bitcast(I32))
        for q in range(4):
            queue = nc.gpsimd if q == 3 else nc.sync
            queue.dma_start(w1s_raw[32 * q : 32 * q + 4, :].bitcast(I32), w1_scales[0, 4 * q : 4 * q + 4, :].bitcast(I32))

        xs_picked = sb("xs_picked", [P, S], U8)
        xs = sb("xs", [P, S], U8)
        xw = sb("xw", [P, S], U32)
        w1w = sb("w1w", [P, 2 * N], U8)
        wa16 = [sb("wa16_%d" % n, [P, PACK * HALF], BF16) for n in range(2)]
        wa_codes = [sb("wa_codes%d" % n, [P, HALF], U32) for n in range(2)]
        wa_scales = [sb("wa_scales%d" % n, [P, HALF], U8) for n in range(2)]
        y16 = sb("y16", [P, PACK, H], BF16)

        def quant_wa(n):
            nc.vector.quantize_mx(out=wa_codes[n][:].bitcast(FP8X4), scales=wa_scales[n][:], in_=wa16[n][:])

        def first(acc, t, n):
            rows = slice(P * t, P * (t + 1))
            nc.tensor.matmul_mx(
                out=acc, lhsT=xw[:, rows].bitcast(FP8X4), lhsT_scale=xs[:, rows],
                rhs=wa_codes[n][:].bitcast(FP8X4), rhs_scale=wa_scales[n][:], start=True, stop=True,
            )

        vc(
            w1w[:].rearrange("p (t m b) -> p t m b", t=PACK, b=2),
            w1w_raw[:].rearrange("p (m t b) -> p t m b", t=PACK, b=2),
        )
        weave(sc, wa16[0][:], wa_raw[0][:])
        vc(xs_picked[:], xs_raw[:].indirect(offs_sb[:]))
        quant_wa(0)
        vc(xs[:].rearrange("p (t m) -> p t m", t=PACK), xs_picked[:].rearrange("p (m t) -> p t m", t=PACK))
        xw_picked = sb("xw_picked", [P, S], U32)
        vc(xw_picked[:], xw_raw[:].indirect(offs_sb[:]))
        split = 160
        weave(sc, wa16[1][:, 0 : PACK * split], wa_raw[1][:, :, 0:split])
        weave(vc, wa16[1][:, PACK * split :], wa_raw[1][:, :, split:])
        vc(
            xw[:].bitcast(I32).rearrange("p (t c i) -> p c t i", t=PACK, i=4),
            xw_picked[:].bitcast(I32).rearrange("p (c i t) -> p c t i", t=PACK, i=4),
        )
        quant_wa(1)
        w1s = sb("w1s", [P, N], U8, "wa16_1")
        vc(w1s[:].rearrange("p (t m) -> p t m", t=PACK), w1s_raw[:].rearrange("p (m t) -> p t m", t=PACK))
        y32 = [sb("y32_%d" % t, [P, H], F32, "wa_raw1" if t == 0 else "") for t in range(PACK)]
        for n in range(2):
            acc = bank("y_acc0_%d" % n)
            first(acc[:, 0:HALF], 0, n)
            nc.scalar.activation(y32[0][:, HALF * n : HALF * (n + 1)], acc[:, 0:HALF], COPY, scale=gt_sb[:, 0:1])
        for t in range(1, PACK):
            acc = bank("y_acc%d" % t)
            for n in range(2):
                first(acc[:, HALF * n : HALF * (n + 1)], t, n)
            nc.scalar.activation(y32[t][:], acc[:], COPY, scale=gt_sb[:, t : t + 1])
        for t in range(PACK):
            sc(y16[:, t, :], y32[t][:])

        out_rows = out_0.rearrange("(p t) h -> p t h", t=PACK)
        out_words = out_1[0].rearrange("p n t -> p (n t)").bitcast(I32)
        o_scales = sb("o_scales", [P, H], U8)

        def gather(dst, lst, t, c0, c1):
            nc.vector.tensor_copy(dst, y32[t][:].indirect(lst[:, c0 // LANES : c1 // LANES]))

        def pick(dst, u, v, op):
            nc.vector.tensor_tensor(dst, u, v, op)

        def quant_z(name, zw, w):
            zc = sb(name + "_codes", [P, w], U32)
            zs = sb(name + "_scales", [P, w], U8)
            nc.vector.quantize_mx(out=zc[:].bitcast(FP8X4), scales=zs[:], in_=zw[:])
            return zc, zs

        def second(name, zq, c0, c1, copies):
            w = c1 - c0
            o32 = sb(name, [P, PACK, w], F32)
            for half in range(2):
                acc = bank("%s_acc%d" % (name, half))
                for u in range(2):
                    t = 2 * half + u
                    nc.tensor.matmul_mx(
                        out=acc[:, u * w : (u + 1) * w],
                        lhsT=w1w[:, 2 * P * t : 2 * P * (t + 1)].bitcast(FP4X4),
                        lhsT_scale=w1s[:, P * t : P * (t + 1)],
                        rhs=zq[0][:].bitcast(FP8X4), rhs_scale=zq[1][:], start=True, stop=True,
                    )
                copies[half](o32[:, 2 * half : 2 * half + 2, :].rearrange("p t w -> p (t w)"), acc[:, 0 : 2 * w])
            nc.sync.dma_start(out_rows[:, :, c0:c1], o32[:])
            return o32

        def round_out(name, copy, o32, w):
            o16 = sb(name, [P, PACK * w], BF16)
            weave(copy, o16[:], o32[:])
            return o16

        def quant_out(name, o16, c0, c1):
            oc = sb(name, [P, c1 - c0], U32)
            nc.vector.quantize_mx(out=oc[:].bitcast(FP8X4), scales=o_scales[:, c0:c1], in_=o16[:])
            nc.sync.dma_start(out_words[:, c0:c1], oc[:].bitcast(I32))

        q3 = HALF + QUARTER
        pairs = (slice(0, 2), slice(2, 4))
        a0 = sb("a0", [P, PACK, HALF], BF16)
        b0 = sb("b0", [P, PACK, HALF], BF16, "picked")
        hi0 = sb("hi0", [P, PACK, HALF], BF16)
        lo0 = sb("lo0", [P, PACK, HALF], BF16)
        z0 = sb("z0", [P, PACK, HALF], BF16, "z0")
        for t in range(PACK):
            gather(a0[:, t, :], fa_sb, t, 0, HALF)
            gather(b0[:, t, :], fb_sb, t, 0, HALF)
        pick(hi0[:], y16[:, :, 0:HALF], a0[:], MAX)
        pick(lo0[:], y16[:, :, 0:HALF], a0[:], MIN)
        for ts in pairs:
            pick(hi0[:, ts, :], hi0[:, ts, :], b0[:, ts, :], MIN)
        for ts in pairs:
            pick(z0[:, ts, :], hi0[:, ts, :], lo0[:, ts, :], MAX)
        zw0 = sb("zw0", [P, PACK * HALF], BF16)
        weave(sc, zw0[:], z0[:])
        a1 = sb("a1", [P, PACK, HALF], BF16, "picked")
        for t in range(PACK):
            gather(a1[:, t, :], fa_sb, t, HALF, H)
        zq0 = quant_z("zq0", zw0, HALF)
        o0 = second("o0", zq0, 0, HALF, (sc, sc))
        o16_0 = round_out("o16_0", sc, o0, HALF)

        work = sb("work", [P, 3, PACK, HALF], BF16, "z0")
        hi1, lo1 = work[:, 0], work[:, 1]
        b1 = work[:, 2].rearrange("p t w -> p (t w)")[:, 0 : PACK * QUARTER].rearrange("p (t w) -> p t w", t=PACK)
        pick(hi1, y16[:, :, HALF:H], a1[:], MAX)
        pick(lo1, y16[:, :, HALF:H], a1[:], MIN)
        for t in range(PACK):
            gather(b1[:, t, :], fb_sb, t, HALF, q3)
        b2a = sb("b2a", [P, 3, QUARTER], BF16, "picked")
        gather(b2a[:, 0, :], fb_sb, 0, q3, H)
        pick(hi1[:, :, 0:QUARTER], hi1[:, :, 0:QUARTER], b1, MIN)
        gather(b2a[:, 1, :], fb_sb, 1, q3, H)
        z1 = sb("z1", [P, PACK, QUARTER], BF16, "z1")
        pick(z1[:], hi1[:, :, 0:QUARTER], lo1[:, :, 0:QUARTER], MAX)
        zw1 = sb("zw1", [P, PACK * QUARTER], BF16)
        weave(sc, zw1[:], z1[:])
        gather(b2a[:, 2, :], fb_sb, 2, q3, H)
        quant_out("oc0", o16_0, 0, HALF)
        pick(hi1[:, 0:3, QUARTER:], hi1[:, 0:3, QUARTER:], b2a[:], MIN)
        zq1 = quant_z("zq1", zw1, QUARTER)
        o1 = second("o1", zq1, HALF, q3, (sc, sc))
        o16_1 = round_out("o16_1", sc, o1, QUARTER)
        last = sb("last", [P, PACK + 1, QUARTER], BF16, "z1")
        z2, b2b = last[:, 0:PACK, :], last[:, PACK, :]
        gather(b2b, fb_sb, 3, q3, H)
        pick(z2[:, 0:3, :], hi1[:, 0:3, QUARTER:], lo1[:, 0:3, QUARTER:], MAX)
        eighth = QUARTER // 2
        parts = (slice(0, eighth), slice(eighth, QUARTER))
        woven = [slice(PACK * c.start, PACK * c.stop) for c in parts]
        hi2, lo2 = hi1[:, 3, QUARTER:], lo1[:, 3, QUARTER:]
        for c in parts:
            pick(hi2[:, c], hi2[:, c], b2b[:, c], MIN)
        for c in parts:
            pick(z2[:, 3, c], hi2[:, c], lo2[:, c], MAX)
        zw2 = sb("zw2", [P, PACK * QUARTER], BF16)
        for c, cw in zip(parts, woven):
            weave(vc, zw2[:, cw], z2[:, :, c])
        zq2 = (sb("zq2_codes", [P, QUARTER], U32), sb("zq2_scales", [P, QUARTER], U8))
        for c, cw in zip(parts, woven):
            nc.vector.quantize_mx(out=zq2[0][:, c].bitcast(FP8X4), scales=zq2[1][:, c], in_=zw2[:, cw])
        quant_out("oc1", o16_1, HALF, q3)
        o2 = second("o2", zq2, q3, H, (vc, sc))
        o16_2 = sb("o16_2", [P, PACK * QUARTER], BF16)
        for c, cw in zip(parts, woven):
            weave(vc, o16_2[:, cw], o2[:, :, c])
        oc2 = sb("oc2", [P, QUARTER], U32)
        for c, cw in zip(parts, woven):
            nc.vector.quantize_mx(
                out=oc2[:, c].bitcast(FP8X4), scales=o_scales[:, q3 + c.start : q3 + c.stop], in_=o16_2[:, cw]
            )
        nc.sync.dma_start(out_words[:, q3:H], oc2[:].bitcast(I32))
        for q in range(4):
            eng = nc.scalar if q % 2 else nc.sync
            eng.dma_start(out_2[0, 4 * q : 4 * q + 4, :].bitcast(I32), o_scales[32 * q : 32 * q + 4, :].bitcast(I32))
